import numpy as np
import ml_dtypes


def mxq(x, axis, fmt="e4m3"):
    dtype, down = {"e4m3": (ml_dtypes.float8_e4m3fn, 7), "e5m2": (ml_dtypes.float8_e5m2, 14)}[fmt]
    v = np.moveaxis(np.asarray(x, np.float32).astype(ml_dtypes.bfloat16).astype(np.float64), axis, -1)
    blocks = v.reshape(v.shape[:-1] + (-1, 32))
    amax = np.abs(blocks).max(-1, keepdims=True)
    byte = np.maximum(np.where(amax > 0, np.frexp(amax)[1] - 1 + 127, 0) - down, 1)
    scale = np.exp2(byte - 127.0)
    codes = (blocks / scale).astype(np.float32).astype(dtype).astype(np.float64)
    return np.moveaxis((codes * scale).reshape(v.shape), -1, axis)


WIDE = False


def mx_kscale(k):
    if not WIDE:
        return np.ones(k)
    levels = np.array([10, -10, 5, -5, 0])
    if k % 512:
        return np.exp2(np.random.permutation(np.resize(levels, k // 32))).repeat(32)
    a = np.empty((k // 512, 16))
    for p in range(k // 512):
        a[p, :8] = np.random.permutation(np.resize(levels, 8))
        for g in range(8):
            far = levels[np.abs(levels - a[p, g]) >= 10]
            a[p, g + 8] = far[np.random.randint(len(far))]
    return np.exp2(a.ravel()).repeat(32)


def f64(x):
    return np.asarray(x).astype(np.float64)


def striped(idx):
    return np.tile(idx.reshape(-1, 16).T, (8, 1)).astype(np.uint16)


def unstriped(offs):
    return offs[:16].T.reshape(-1).astype(np.int64)


def striped8(idx):
    return np.concatenate([x.reshape(-1, 16).T for x in idx]).astype(np.uint16)


def runs(offs, k):
    lists = np.stack([offs[16 * r : 16 * r + 16].T.reshape(-1) for r in range(8)]).astype(np.int64)
    return lists[np.arange(k) % 512 // 64]


def pack_weight(w):
    k, n = w.shape
    w = f64(np.asarray(w, np.float32).astype(ml_dtypes.bfloat16)).reshape(k // 32, 32, n)
    amax = np.abs(w).max(1)
    byte = np.clip(np.where(amax > 0, np.frexp(amax)[1] - 1 + 127 - 7, 1), 1, 254)
    scaled = (w * np.exp2(127.0 - byte)[:, None, :]).reshape(k, n).astype(np.float32)
    words = np.ascontiguousarray(scaled.reshape(k // 512, 128, 4, n).transpose(0, 1, 3, 2)).astype(ml_dtypes.float8_e4m3fn).view(np.uint8)
    return words, np.ascontiguousarray(byte.astype(np.uint8).reshape(k // 512, 16, n))


def unpack_weight(words, scales):
    g, p, n, _ = words.shape
    vals = np.ascontiguousarray(words).view(ml_dtypes.float8_e4m3fn).astype(np.float64) * np.repeat(np.exp2(scales.astype(np.float64) - 127.0), 8, axis=1)[..., None]
    return vals.transpose(0, 1, 3, 2).reshape(g * 512, n)


def sigmoid(v):
    return 1.0 / (1.0 + np.exp(-np.maximum(v, -700.0)))


K, T, S, V, H, C = 512, 2048, 1024, 512, 512, 512


def setup_inputs():
    n = np.random.standard_normal
    s = mx_kscale(K)[:, None]
    packed_xT = pack_weight(n((K, T)) * s)
    return {
        "x_words": packed_xT[0],
        "x_scales": packed_xT[1],
        "w1": (n((K, H)) / np.sqrt(K) / s).astype(np.float32),
        "gs": (np.random.uniform(0.5, 1.5, (K, 1)) / s).astype(np.float32),
        "offs": striped(np.random.permutation(T)[:S]),
        "n1": striped8(np.stack([np.random.permutation(S) for _ in range(8)])),
        "cand": striped(np.random.permutation(T)[:C]),
        "n2": striped8(np.stack([np.random.permutation(V) for _ in range(8)])),
    }


def reference(x_words, x_scales, w1, gs, offs, n1, cand, n2):
    x_cand = unpack_weight(x_words, x_scales)[:, unstriped(cand)]
    xq = unpack_weight(x_words, x_scales)[:, unstriped(offs)]
    y = mxq(f64(w1), 0, "e4m3").T @ xq
    ln = y[np.arange(H)[:, None], runs(n1, H)]
    sq = (ln) ** 2
    ms = sq.reshape(H, V, 2).sum(axis=2)
    z = f64(gs) * np.sqrt(ms + 0.1)
    s = 0.0625 * ((x_cand.T @ mxq(z, 0, "e4m3")))
    st = s * (sigmoid(s[np.arange(C)[:, None], runs(n2, C)]))
    return np.maximum(st, st[np.arange(C)[:, None], runs(n2, C)])

@@ -1,0 +1,168 @@
+from contextlib import ExitStack
+
+import concourse.mybir as mybir
+
+K, T, S, V, H, C = 512, 2048, 1024, 512, 512, 512
+FLOPS = 2 * K * H * S + 2 * H * C * V
+
+F32 = mybir.dt.float32
+BF16 = mybir.dt.bfloat16
+I32 = mybir.dt.int32
+U32 = mybir.dt.uint32
+U16 = mybir.dt.uint16
+U8 = mybir.dt.uint8
+FP8X4 = mybir.dt.float8_e4m3fn_x4
+ACT = mybir.ActivationFunctionType
+ALU = mybir.AluOpType
+
+P = 128
+PACK = 4
+BANK = 512
+CHUNKS = ((0, 256), (256, 128), (384, 128))
+HALF = V // 2
+
+
+def tile_picked_candprmstwicp_none_p_kernel(tc, x_words, x_scales, w1, gs, offs, n1, cand, n2, out):
+    nc = tc.nc
+    with ExitStack() as ctx:
+        keep = ctx.enter_context(tc.tile_pool(name="keep", bufs=1))
+        psum = ctx.enter_context(tc.psum_pool(name="psum", bufs=8))
+
+        offs_t = keep.tile([P, S // 16], U16, name="offs_t")
+        cand_t = keep.tile([P, C // 16], U16, name="cand_t")
+        n1_t = keep.tile([P, S // 16], U16, name="n1_t")
+        n2_t = keep.tile([P, V // 16], U16, name="n2_t")
+        x_bytes = keep.tile([P, T], U8, name="x_bytes", align_bytes=64)
+        x_codes = keep.tile([P, T], I32, name="x_codes", tag="x_codes", align_bytes=64)
+        w_raw = [keep.tile([P, PACK, H // 2], F32, name="w_raw%d" % h, align_bytes=64) for h in range(2)]
+        gain = keep.tile([P, PACK], F32, name="gain")
+        warm = keep.tile([P, 8], F32, name="warm")
+
+        nc.gpsimd.memset(x_bytes[:].bitcast(I32), 0)
+        nc.gpsimd.memset(warm[:], 1.0)
+        nc.scalar.activation(warm[:, 1:2], warm[:, 0:1], ACT.Sqrt)
+        nc.sync.dma_start(offs_t[:], offs)
+        nc.sync.dma_start(cand_t[:], cand)
+        for q in range(4):
+            nc.sync.dma_start(x_bytes[32 * q : 32 * q + 4, :].bitcast(I32), x_scales[0, 4 * q : 4 * q + 4, :].bitcast(I32))
+        w_rows = w1.rearrange("(p j) c -> p j c", j=PACK)
+        for h in range(2):
+            nc.sync.dma_start(w_raw[h][:], w_rows[:, :, H // 2 * h : H // 2 * (h + 1)])
+        nc.sync.dma_start(x_codes[:], x_words[0].rearrange("p n r -> p (n r)").bitcast(I32))
+        nc.sync.dma_start(n1_t[:], n1)
+        nc.sync.dma_start(gain[:], gs.rearrange("(p t) o -> p (t o)", t=PACK))
+        nc.sync.dma_start(n2_t[:], n2)
+
+        tok_scales = keep.tile([P, S], U8, name="tok_scales", align_bytes=64)
+        nc.vector.tensor_copy(tok_scales[:], x_bytes[:].indirect(offs_t[:]))
+        cand_bytes = keep.tile([P, C], U8, name="cand_bytes", align_bytes=64)
+        nc.vector.tensor_copy(cand_bytes[:], x_bytes[:].indirect(cand_t[:]))
+
+        w_bf = keep.tile([P, PACK * H], BF16, name="w_bf", align_bytes=64)
+        w_dealt = w_bf[:].rearrange("p (t m j) -> p m j t", t=PACK, j=PACK)
+        for h in range(2):
+            nc.scalar.copy(w_dealt[:, P // 2 * h : P // 2 * (h + 1)], w_raw[h][:].rearrange("p j (m t) -> p m j t", t=PACK))
+        w_codes = keep.tile([P, H], U32, name="w_codes", align_bytes=64)
+        w_scales = keep.tile([P, H], U8, name="w_scales", align_bytes=64)
+        nc.vector.quantize_mx(out=w_codes[:].bitcast(FP8X4), scales=w_scales[:], in_=w_bf[:])
+
+        tok_codes = []
+        for h in range(2):
+            codes = keep.tile([P, BANK], U32, name="tok_codes%d" % h, align_bytes=64)
+            nc.vector.tensor_copy(codes[:], x_codes[:].bitcast(U32).indirect(offs_t[:, 32 * h : 32 * h + 32]))
+            tok_codes.append(codes)
+        cand_codes = keep.tile([P, C], U32, name="cand_codes", align_bytes=64)
+        nc.vector.tensor_copy(
+            cand_codes[:].rearrange("p (t m) -> p m t", t=PACK), x_codes[:].bitcast(U32).indirect(cand_t[:])
+        )
+        cand_scales = keep.tile([P, C], U8, name="cand_scales", tag="x_codes", align_bytes=64)
+        nc.vector.tensor_copy(
+            cand_scales[:].rearrange("p (t m) -> p t m", t=PACK), cand_bytes[:].rearrange("p (m t) -> p t m", t=PACK)
+        )
+
+        squares = []
+        for t in range(PACK):
+            cols = slice(P * t, P * t + P)
+            sq = keep.tile([P, S], F32, name="sq%d" % t, align_bytes=64)
+            for h in range(2):
+                acc = psum.tile([P, BANK], F32, name="acc", tag="bank")
+                nc.tensor.matmul_mx(
+                    out=acc[:],
+                    lhsT=w_codes[:, cols].bitcast(FP8X4),
+                    lhsT_scale=w_scales[:, cols],
+                    rhs=tok_codes[h][:].bitcast(FP8X4),
+                    rhs_scale=tok_scales[:, BANK * h : BANK * h + BANK],
+                    start=True,
+                    stop=True,
+                )
+                nc.scalar.activation(sq[:, BANK * h : BANK * h + BANK], acc[:], ACT.Square)
+            squares.append(sq)
+
+        scores = [psum.tile([P, V], F32, name="score%d" % u, tag="bank") for u in range(PACK)]
+        planes = [keep.tile([P, PACK, n], BF16, name="planes%d" % c, align_bytes=64) for c, (v0, n) in enumerate(CHUNKS)]
+        for t in range(PACK):
+            lined = keep.tile([P, S], F32, name="lined%d" % t, align_bytes=64)
+            ms = keep.tile([P, V], F32, name="ms%d" % t, align_bytes=64)
+            root = keep.tile([P, V], F32, name="root%d" % t, align_bytes=64)
+            pairs = lined[:].rearrange("p (v e) -> p v e", e=2)
+            fetches = CHUNKS if t == PACK - 1 else ((0, HALF), (HALF, HALF))
+            steps = CHUNKS if t == PACK - 1 else ((0, V),)
+            for v0, n in fetches:
+                nc.vector.tensor_copy(lined[:, 2 * v0 : 2 * (v0 + n)], squares[t][:].indirect(n1_t[:, v0 // 8 : (v0 + n) // 8]))
+            for v0, n in steps:
+                vs = slice(v0, v0 + n)
+                nc.vector.tensor_tensor(ms[:, vs], pairs[:, vs, 0], pairs[:, vs, 1], ALU.add)
+                nc.scalar.activation(root[:, vs], ms[:, vs], ACT.Sqrt, bias=0.1)
+                for c, (c0, cn) in enumerate(CHUNKS):
+                    if v0 <= c0 < v0 + n:
+                        nc.scalar.activation(planes[c][:, t, :], root[:, c0 : c0 + cn], ACT.Copy, scale=gain[:, t : t + 1])
+        nc.scalar.activation(warm[:, 2:3], planes[-1][:, PACK - 1, 0:1], ACT.Sigmoid)
+        for c, (v0, n) in enumerate(CHUNKS):
+            z_bf = keep.tile([P, n, PACK], BF16, name="z_bf%d" % c, align_bytes=64)
+            nc.vector.tensor_copy(
+                z_bf[:].rearrange("p (c i) t -> p c t i", i=4), planes[c][:].rearrange("p t (c i) -> p c t i", i=4)
+            )
+            z_codes = keep.tile([P, n], U32, name="z_codes%d" % c, align_bytes=64)
+            z_scales = keep.tile([P, n], U8, name="z_scales%d" % c, align_bytes=64)
+            nc.vector.quantize_mx(
+                out=z_codes[:].bitcast(FP8X4), scales=z_scales[:], in_=z_bf[:].rearrange("p v t -> p (v t)")
+            )
+            for u in range(PACK):
+                cols = slice(P * u, P * u + P)
+                nc.tensor.matmul_mx(
+                    out=scores[u][:, v0 : v0 + n],
+                    lhsT=cand_codes[:, cols].bitcast(FP8X4),
+                    lhsT_scale=cand_scales[:, cols],
+                    rhs=z_codes[:].bitcast(FP8X4),
+                    rhs_scale=z_scales[:],
+                    start=True,
+                    stop=True,
+                )
+
+        rows = out.rearrange("(p u) v -> p u v", u=PACK)
+        halves = [slice(0, HALF), slice(HALF, V)]
+        lists = [n2_t[:, 0 : HALF // 16], n2_t[:, HALF // 16 : V // 16]]
+        for u in range(PACK):
+            s = keep.tile([P, V], F32, name="s%d" % u, align_bytes=64)
+            if u % 2 == 0:
+                nc.vector.tensor_scalar_mul(s[:], scores[u][:], 0.0625)
+            else:
+                nc.scalar.mul(s[:], scores[u][:], 0.0625)
+            both = keep.tile([P, 2 * V], F32, name="both%d" % u, align_bytes=64)
+            st, gate = both[:, 0:V], both[:, V : 2 * V]
+            other = keep.tile([P, V], F32, name="other%d" % u, align_bytes=64)
+            res = keep.tile([P, V], F32, name="res%d" % u, align_bytes=64)
+            for h in range(2):
+                nc.scalar.activation(gate[:, halves[h]], s[:].indirect(lists[h]), ACT.Sigmoid)
+            for vs in halves if u == 0 else [slice(0, V)]:
+                nc.vector.tensor_tensor(st[:, vs], s[:, vs], gate[:, vs], ALU.mult)
+            if u < PACK - 1:
+                nc.vector.tensor_copy(other[:], both[:].indirect(n2_t[:]))
+                nc.vector.tensor_tensor(res[:], st, other[:], ALU.max)
+                nc.sync.dma_start(rows[:, u, :], res[:])
+            else:
+                for h in range(2):
+                    nc.vector.tensor_copy(other[:, halves[h]], both[:].indirect(lists[h]))
+                for h in range(2):
+                    nc.vector.tensor_tensor(res[:, halves[h]], st[:, halves[h]], other[:, halves[h]], ALU.max)
+                    nc.sync.dma_start(rows[:, u, halves[h]], res[:, halves[h]])

@@ -38,7 +38,7 @@ def tile_picked_candprmstwicp_none_p_kernel(tc, x_words, x_scales, w1, gs, offs,
         gain = keep.tile([P, PACK], F32, name="gain")
         warm = keep.tile([P, 8], F32, name="warm")
 
-        nc.gpsimd.memset(x_bytes[:].bitcast(I32), 0)
+        nc.vector.memset(x_bytes[:].bitcast(I32), 0)
         nc.gpsimd.memset(warm[:], 1.0)
         nc.scalar.activation(warm[:, 1:2], warm[:, 0:1], ACT.Sqrt)
         nc.sync.dma_start(offs_t[:], offs)
@@ -68,22 +68,18 @@ def tile_picked_candprmstwicp_none_p_kernel(tc, x_words, x_scales, w1, gs, offs,
 
         tok_codes = []
         for h in range(2):
-            codes = keep.tile([P, BANK], U32, name="tok_codes%d" % h, align_bytes=64)
+            codes = keep.tile([P, BANK], U32, name="tok_codes%d" % h, tag="tok_codes%d" % h, align_bytes=64)
             nc.vector.tensor_copy(codes[:], x_codes[:].bitcast(U32).indirect(offs_t[:, 32 * h : 32 * h + 32]))
             tok_codes.append(codes)
         cand_codes = keep.tile([P, C], U32, name="cand_codes", align_bytes=64)
         nc.vector.tensor_copy(
             cand_codes[:].rearrange("p (t m) -> p m t", t=PACK), x_codes[:].bitcast(U32).indirect(cand_t[:])
         )
-        cand_scales = keep.tile([P, C], U8, name="cand_scales", tag="x_codes", align_bytes=64)
-        nc.vector.tensor_copy(
-            cand_scales[:].rearrange("p (t m) -> p t m", t=PACK), cand_bytes[:].rearrange("p (m t) -> p t m", t=PACK)
-        )
 
         squares = []
         for t in range(PACK):
             cols = slice(P * t, P * t + P)
-            sq = keep.tile([P, S], F32, name="sq%d" % t, align_bytes=64)
+            sq = keep.tile([P, S], F32, name="sq%d" % t, tag="sq%d" % t, align_bytes=64)
             for h in range(2):
                 acc = psum.tile([P, BANK], F32, name="acc", tag="bank")
                 nc.tensor.matmul_mx(
@@ -99,28 +95,32 @@ def tile_picked_candprmstwicp_none_p_kernel(tc, x_words, x_scales, w1, gs, offs,
             squares.append(sq)
 
         scores = [psum.tile([P, V], F32, name="score%d" % u, tag="bank") for u in range(PACK)]
-        planes = [keep.tile([P, PACK, n], BF16, name="planes%d" % c, align_bytes=64) for c, (v0, n) in enumerate(CHUNKS)]
+        planes = [keep.tile([P, 2, n, 2], BF16, name="planes%d" % c, align_bytes=64) for c, (v0, n) in enumerate(CHUNKS)]
         for t in range(PACK):
             lined = keep.tile([P, S], F32, name="lined%d" % t, align_bytes=64)
             ms = keep.tile([P, V], F32, name="ms%d" % t, align_bytes=64)
-            root = keep.tile([P, V], F32, name="root%d" % t, align_bytes=64)
+            root = keep.tile([P, V], F32, name="root%d" % t, tag="tok_codes1" if t == 0 else "root%d" % t, align_bytes=64)
             pairs = lined[:].rearrange("p (v e) -> p v e", e=2)
             fetches = CHUNKS if t == PACK - 1 else ((0, HALF), (HALF, HALF))
-            steps = CHUNKS if t == PACK - 1 else ((0, V),)
             for v0, n in fetches:
                 nc.vector.tensor_copy(lined[:, 2 * v0 : 2 * (v0 + n)], squares[t][:].indirect(n1_t[:, v0 // 8 : (v0 + n) // 8]))
-            for v0, n in steps:
+            for v0, n in fetches:
                 vs = slice(v0, v0 + n)
-                nc.vector.tensor_tensor(ms[:, vs], pairs[:, vs, 0], pairs[:, vs, 1], ALU.add)
+                (nc.vector if (t, v0 + n) == (PACK - 1, V) else nc.gpsimd).tensor_tensor(ms[:, vs], pairs[:, vs, 0], pairs[:, vs, 1], ALU.add)
                 nc.scalar.activation(root[:, vs], ms[:, vs], ACT.Sqrt, bias=0.1)
                 for c, (c0, cn) in enumerate(CHUNKS):
                     if v0 <= c0 < v0 + n:
-                        nc.scalar.activation(planes[c][:, t, :], root[:, c0 : c0 + cn], ACT.Copy, scale=gain[:, t : t + 1])
-        nc.scalar.activation(warm[:, 2:3], planes[-1][:, PACK - 1, 0:1], ACT.Sigmoid)
+                        nc.scalar.activation(planes[c][:, t // 2, :, t % 2], root[:, c0 : c0 + cn], ACT.Copy, scale=gain[:, t : t + 1])
+        cand_scales = keep.tile([P, C], U8, name="cand_scales", tag="sq3", align_bytes=64)
+        nc.vector.tensor_copy(
+            cand_scales[:].rearrange("p (t m) -> p t m", t=PACK), cand_bytes[:].rearrange("p (m t) -> p t m", t=PACK)
+        )
+        nc.scalar.activation(warm[:, 2:3], planes[-1][:, 1, 0, 1:2], ACT.Sigmoid)
         for c, (v0, n) in enumerate(CHUNKS):
             z_bf = keep.tile([P, n, PACK], BF16, name="z_bf%d" % c, align_bytes=64)
             nc.vector.tensor_copy(
-                z_bf[:].rearrange("p (c i) t -> p c t i", i=4), planes[c][:].rearrange("p t (c i) -> p c t i", i=4)
+                z_bf[:].rearrange("p v t -> p (v t)").bitcast(F32).rearrange("p (c i u) -> p c u i", i=4, u=2),
+                planes[c][:].rearrange("p u v e -> p (u v e)").bitcast(F32).rearrange("p (u c i) -> p c u i", i=4, u=2),
             )
             z_codes = keep.tile([P, n], U32, name="z_codes%d" % c, align_bytes=64)
             z_scales = keep.tile([P, n], U8, name="z_scales%d" % c, align_bytes=64)
@@ -144,7 +144,7 @@ def tile_picked_candprmstwicp_none_p_kernel(tc, x_words, x_scales, w1, gs, offs,
         lists = [n2_t[:, 0 : HALF // 16], n2_t[:, HALF // 16 : V // 16]]
         for u in range(PACK):
             s = keep.tile([P, V], F32, name="s%d" % u, align_bytes=64)
-            if u % 2 == 0:
+            if u < 2:
                 nc.vector.tensor_scalar_mul(s[:], scores[u][:], 0.0625)
             else:
                 nc.scalar.mul(s[:], scores[u][:], 0.0625)
@@ -154,8 +154,8 @@ def tile_picked_candprmstwicp_none_p_kernel(tc, x_words, x_scales, w1, gs, offs,
             res = keep.tile([P, V], F32, name="res%d" % u, align_bytes=64)
             for h in range(2):
                 nc.scalar.activation(gate[:, halves[h]], s[:].indirect(lists[h]), ACT.Sigmoid)
-            for vs in halves if u == 0 else [slice(0, V)]:
-                nc.vector.tensor_tensor(st[:, vs], s[:, vs], gate[:, vs], ALU.mult)
+            for vs in halves:
+                (nc.vector if u == 0 else nc.gpsimd).tensor_tensor(st[:, vs], s[:, vs], gate[:, vs], ALU.mult)
             if u < PACK - 1:
                 nc.vector.tensor_copy(other[:], both[:].indirect(n2_t[:]))
                 nc.vector.tensor_tensor(res[:], st, other[:], ALU.max)

@@ -20,13 +20,15 @@ PACK = 4
 BANK = 512
 CHUNKS = ((0, 256), (256, 128), (384, 128))
 HALF = V // 2
+TOK_PARTS = ((0, 512), (512, 768), (768, 1024))
+W_PARTS = ((0, 192), (192, 384), (384, 512))
 
 
 def tile_picked_candprmstwicp_none_p_kernel(tc, x_words, x_scales, w1, gs, offs, n1, cand, n2, out):
     nc = tc.nc
     with ExitStack() as ctx:
         keep = ctx.enter_context(tc.tile_pool(name="keep", bufs=1))
-        psum = ctx.enter_context(tc.psum_pool(name="psum", bufs=8))
+        psum = ctx.enter_context(tc.psum_pool(name="psum", bufs=1))
 
         offs_t = keep.tile([P, S // 16], U16, name="offs_t")
         cand_t = keep.tile([P, C // 16], U16, name="cand_t")
@@ -34,7 +36,7 @@ def tile_picked_candprmstwicp_none_p_kernel(tc, x_words, x_scales, w1, gs, offs,
         n2_t = keep.tile([P, V // 16], U16, name="n2_t")
         x_bytes = keep.tile([P, T], U8, name="x_bytes", align_bytes=64)
         x_codes = keep.tile([P, T], I32, name="x_codes", tag="x_codes", align_bytes=64)
-        w_raw = [keep.tile([P, PACK, H // 2], F32, name="w_raw%d" % h, align_bytes=64) for h in range(2)]
+        w_raw = [keep.tile([P, PACK, c1 - c0], F32, name="w_raw%d" % c0, tag="w_raw%d" % c0, align_bytes=64) for c0, c1 in W_PARTS]
         gain = keep.tile([P, PACK], F32, name="gain")
         warm = keep.tile([P, 8], F32, name="warm")
 
@@ -46,9 +48,10 @@ def tile_picked_candprmstwicp_none_p_kernel(tc, x_words, x_scales, w1, gs, offs,
         for q in range(4):
             nc.sync.dma_start(x_bytes[32 * q : 32 * q + 4, :].bitcast(I32), x_scales[0, 4 * q : 4 * q + 4, :].bitcast(I32))
         w_rows = w1.rearrange("(p j) c -> p j c", j=PACK)
-        for h in range(2):
-            nc.sync.dma_start(w_raw[h][:], w_rows[:, :, H // 2 * h : H // 2 * (h + 1)])
-        nc.sync.dma_start(x_codes[:], x_words[0].rearrange("p n r -> p (n r)").bitcast(I32))
+        for i, (c0, c1) in enumerate(W_PARTS):
+            nc.sync.dma_start(w_raw[i][:], w_rows[:, :, c0:c1])
+            if i == 0:
+                nc.sync.dma_start(x_codes[:], x_words[0].rearrange("p n r -> p (n r)").bitcast(I32))
         nc.sync.dma_start(n1_t[:], n1)
         nc.sync.dma_start(gain[:], gs.rearrange("(p t) o -> p (t o)", t=PACK))
         nc.sync.dma_start(n2_t[:], n2)
@@ -58,22 +61,35 @@ def tile_picked_candprmstwicp_none_p_kernel(tc, x_words, x_scales, w1, gs, offs,
         cand_bytes = keep.tile([P, C], U8, name="cand_bytes", align_bytes=64)
         nc.vector.tensor_copy(cand_bytes[:], x_bytes[:].indirect(cand_t[:]))
 
-        w_bf = keep.tile([P, PACK * H], BF16, name="w_bf", align_bytes=64)
+        w_bf = keep.tile([P, PACK * H], BF16, name="w_bf", tag="w_bf", align_bytes=64)
         w_dealt = w_bf[:].rearrange("p (t m j) -> p m j t", t=PACK, j=PACK)
-        for h in range(2):
-            nc.scalar.copy(w_dealt[:, P // 2 * h : P // 2 * (h + 1)], w_raw[h][:].rearrange("p j (m t) -> p m j t", t=PACK))
+        for i, (c0, c1) in enumerate(W_PARTS):
+            nc.scalar.copy(w_dealt[:, c0 // PACK : c1 // PACK], w_raw[i][:].rearrange("p j (m t) -> p m j t", t=PACK))
         w_codes = keep.tile([P, H], U32, name="w_codes", align_bytes=64)
         w_scales = keep.tile([P, H], U8, name="w_scales", align_bytes=64)
-        nc.vector.quantize_mx(out=w_codes[:].bitcast(FP8X4), scales=w_scales[:], in_=w_bf[:])
+
+        def quantize_w(h):
+            cols = slice(H // 2 * h, H // 2 * (h + 1))
+            nc.vector.quantize_mx(
+                out=w_codes[:, cols].bitcast(FP8X4), scales=w_scales[:, cols], in_=w_bf[:, 2 * H * h : 2 * H * (h + 1)]
+            )
+
+        quantize_w(0)
 
         tok_codes = []
-        for h in range(2):
-            codes = keep.tile([P, BANK], U32, name="tok_codes%d" % h, tag="tok_codes%d" % h, align_bytes=64)
-            nc.vector.tensor_copy(codes[:], x_codes[:].bitcast(U32).indirect(offs_t[:, 32 * h : 32 * h + 32]))
+        for h, (j0, j1) in enumerate(TOK_PARTS):
+            codes = keep.tile([P, j1 - j0], U32, name="tok_codes%d" % h, tag=("tok_codes0", "tok_codes1", "w_raw384")[h], align_bytes=64)
+            nc.vector.tensor_copy(codes[:], x_codes[:].bitcast(U32).indirect(offs_t[:, j0 // 16 : j1 // 16]))
             tok_codes.append(codes)
-        cand_codes = keep.tile([P, C], U32, name="cand_codes", align_bytes=64)
+        quantize_w(1)
+        cand_codes = keep.tile([P, C], U32, name="cand_codes", tag="w_bf", align_bytes=64)
         nc.vector.tensor_copy(
-            cand_codes[:].rearrange("p (t m) -> p m t", t=PACK), x_codes[:].bitcast(U32).indirect(cand_t[:])
+            cand_codes[:].rearrange("p (u a c) -> p a u c", u=PACK, c=4), x_codes[:].bitcast(U32).indirect(cand_t[:])
+        )
+        cand_scales = keep.tile([P, C], U8, name="cand_scales", tag="x_codes", align_bytes=64)
+        nc.vector.tensor_copy(
+            cand_scales[:].bitcast(I32).rearrange("p (u a) -> p u a", u=PACK),
+            cand_bytes[:].bitcast(I32).rearrange("p (a u) -> p u a", u=PACK),
         )
 
         squares = []
@@ -81,56 +97,72 @@ def tile_picked_candprmstwicp_none_p_kernel(tc, x_words, x_scales, w1, gs, offs,
             cols = slice(P * t, P * t + P)
             sq = keep.tile([P, S], F32, name="sq%d" % t, tag="sq%d" % t, align_bytes=64)
             for h in range(2):
-                acc = psum.tile([P, BANK], F32, name="acc", tag="bank")
-                nc.tensor.matmul_mx(
-                    out=acc[:],
-                    lhsT=w_codes[:, cols].bitcast(FP8X4),
-                    lhsT_scale=w_scales[:, cols],
-                    rhs=tok_codes[h][:].bitcast(FP8X4),
-                    rhs_scale=tok_scales[:, BANK * h : BANK * h + BANK],
-                    start=True,
-                    stop=True,
-                )
+                acc = psum.tile([P, BANK], F32, name="acc", tag="acc", bufs=5)
+                for codes, (j0, j1) in zip(tok_codes, TOK_PARTS):
+                    if j0 // BANK == h:
+                        nc.tensor.matmul_mx(
+                            out=acc[:, j0 - BANK * h : j1 - BANK * h],
+                            lhsT=w_codes[:, cols].bitcast(FP8X4),
+                            lhsT_scale=w_scales[:, cols],
+                            rhs=codes[:].bitcast(FP8X4),
+                            rhs_scale=tok_scales[:, j0:j1],
+                            start=True,
+                            stop=True,
+                        )
                 nc.scalar.activation(sq[:, BANK * h : BANK * h + BANK], acc[:], ACT.Square)
             squares.append(sq)
 
-        scores = [psum.tile([P, V], F32, name="score%d" % u, tag="bank") for u in range(PACK)]
         planes = [keep.tile([P, 2, n, 2], BF16, name="planes%d" % c, align_bytes=64) for c, (v0, n) in enumerate(CHUNKS)]
-        for t in range(PACK):
-            lined = keep.tile([P, S], F32, name="lined%d" % t, align_bytes=64)
-            ms = keep.tile([P, V], F32, name="ms%d" % t, align_bytes=64)
-            root = keep.tile([P, V], F32, name="root%d" % t, tag="tok_codes1" if t == 0 else "root%d" % t, align_bytes=64)
+        z_bfs = [keep.tile([P, n, PACK], BF16, name="z_bf%d" % c, tag="z_bf%d" % c, align_bytes=64) for c, (v0, n) in enumerate(CHUNKS)]
+        sums = [keep.tile([P, V], F32, name="ms%d" % t, align_bytes=64) for t in range(PACK)]
+        roots = [
+            keep.tile([P, V], F32, name="root%d" % t, tag="w_raw384" if t == 0 else "root%d" % t, align_bytes=64)
+            for t in range(PACK)
+        ]
+        order = [(0, 0), (0, 1), (1, 0), (1, 1), (2, 0), (3, 0), (3, 1), (2, 1)]
+        for t, h in order:
+            final = (t, h) == order[-1]
+            lined = keep.tile([P, BANK], F32, name="lined%d%d" % (t, h), tag="lined30" if final else "lined%d%d" % (t, h), align_bytes=64)
             pairs = lined[:].rearrange("p (v e) -> p v e", e=2)
-            fetches = CHUNKS if t == PACK - 1 else ((0, HALF), (HALF, HALF))
-            for v0, n in fetches:
-                nc.vector.tensor_copy(lined[:, 2 * v0 : 2 * (v0 + n)], squares[t][:].indirect(n1_t[:, v0 // 8 : (v0 + n) // 8]))
-            for v0, n in fetches:
+            pieces = CHUNKS[1:] if final else ((HALF * h, HALF),)
+            for v0, n in pieces:
+                u0 = v0 - HALF * h
+                nc.vector.tensor_copy(lined[:, 2 * u0 : 2 * (u0 + n)], squares[t][:].indirect(n1_t[:, v0 // 8 : (v0 + n) // 8]))
+            for v0, n in pieces:
                 vs = slice(v0, v0 + n)
-                (nc.vector if (t, v0 + n) == (PACK - 1, V) else nc.gpsimd).tensor_tensor(ms[:, vs], pairs[:, vs, 0], pairs[:, vs, 1], ALU.add)
-                nc.scalar.activation(root[:, vs], ms[:, vs], ACT.Sqrt, bias=0.1)
+                us = slice(v0 - HALF * h, v0 - HALF * h + n)
+                adder = nc.vector if final and v0 + n == V else nc.gpsimd
+                adder.tensor_tensor(sums[t][:, vs], pairs[:, us, 0], pairs[:, us, 1], ALU.add)
+                nc.scalar.activation(roots[t][:, vs], sums[t][:, vs], ACT.Sqrt, bias=0.1)
                 for c, (c0, cn) in enumerate(CHUNKS):
                     if v0 <= c0 < v0 + n:
-                        nc.scalar.activation(planes[c][:, t // 2, :, t % 2], root[:, c0 : c0 + cn], ACT.Copy, scale=gain[:, t : t + 1])
-        cand_scales = keep.tile([P, C], U8, name="cand_scales", tag="sq3", align_bytes=64)
-        nc.vector.tensor_copy(
-            cand_scales[:].rearrange("p (t m) -> p t m", t=PACK), cand_bytes[:].rearrange("p (m t) -> p t m", t=PACK)
-        )
-        nc.scalar.activation(warm[:, 2:3], planes[-1][:, 1, 0, 1:2], ACT.Sigmoid)
+                        target = planes[c][:, t // 2, :, t % 2] if c < len(planes) else z_bfs[c][:, :, t]
+                        nc.scalar.activation(target, roots[t][:, c0 : c0 + cn], ACT.Copy, scale=gain[:, t : t + 1])
+        nc.scalar.activation(warm[:, 2:3], planes[-1][:, 1, 0, 0:1], ACT.Sigmoid)
+        z_mx = []
         for c, (v0, n) in enumerate(CHUNKS):
-            z_bf = keep.tile([P, n, PACK], BF16, name="z_bf%d" % c, align_bytes=64)
-            nc.vector.tensor_copy(
-                z_bf[:].rearrange("p v t -> p (v t)").bitcast(F32).rearrange("p (c i u) -> p c u i", i=4, u=2),
-                planes[c][:].rearrange("p u v e -> p (u v e)").bitcast(F32).rearrange("p (u c i) -> p c u i", i=4, u=2),
-            )
+            z_bf = z_bfs[c]
+            if c < len(planes):
+                nc.vector.tensor_copy(
+                    z_bf[:].rearrange("p v t -> p (v t)").bitcast(F32).rearrange("p (c i u) -> p c u i", i=4, u=2),
+                    planes[c][:].rearrange("p u v e -> p (u v e)").bitcast(F32).rearrange("p (u c i) -> p c u i", i=4, u=2),
+                )
             z_codes = keep.tile([P, n], U32, name="z_codes%d" % c, align_bytes=64)
             z_scales = keep.tile([P, n], U8, name="z_scales%d" % c, align_bytes=64)
             nc.vector.quantize_mx(
                 out=z_codes[:].bitcast(FP8X4), scales=z_scales[:], in_=z_bf[:].rearrange("p v t -> p (v t)")
             )
-            for u in range(PACK):
-                cols = slice(P * u, P * u + P)
+            z_mx.append((z_codes, z_scales))
+        rows = out.rearrange("(a u c) v -> u c a v", u=PACK, c=4)
+        halves = [slice(0, HALF), slice(HALF, V)]
+        lists = [n2_t[:, 0 : HALF // 16], n2_t[:, HALF // 16 : V // 16]]
+        late = psum.tile([P, V], F32, name="late", tag="late")
+        for u in range(PACK):
+            cols = slice(P * u, P * u + P)
+            score = psum.tile([P, V], F32, name="score%d" % u, tag=("first", "second", "late", "first")[u])
+            for (v0, n), (z_codes, z_scales) in zip(CHUNKS, z_mx):
                 nc.tensor.matmul_mx(
-                    out=scores[u][:, v0 : v0 + n],
+                    out=(late if (u, v0 + n) == (0, V) else score)[:, v0 : v0 + n],
                     lhsT=cand_codes[:, cols].bitcast(FP8X4),
                     lhsT_scale=cand_scales[:, cols],
                     rhs=z_codes[:].bitcast(FP8X4),
@@ -138,31 +170,26 @@ def tile_picked_candprmstwicp_none_p_kernel(tc, x_words, x_scales, w1, gs, offs,
                     start=True,
                     stop=True,
                 )
-
-        rows = out.rearrange("(p u) v -> p u v", u=PACK)
-        halves = [slice(0, HALF), slice(HALF, V)]
-        lists = [n2_t[:, 0 : HALF // 16], n2_t[:, HALF // 16 : V // 16]]
-        for u in range(PACK):
-            s = keep.tile([P, V], F32, name="s%d" % u, align_bytes=64)
-            if u < 2:
-                nc.vector.tensor_scalar_mul(s[:], scores[u][:], 0.0625)
+            s = keep.tile([P, V], F32, name="s%d" % u, tag=("z_bf2", "s1", "z_bf2", "both0")[u], align_bytes=64)
+            if u == 0:
+                cut = CHUNKS[-1][0]
+                nc.vector.tensor_scalar_mul(s[:, 0:cut], score[:, 0:cut], 0.0625)
+                nc.vector.tensor_scalar_mul(s[:, cut:V], late[:, cut:V], 0.0625)
+            elif u == 1:
+                nc.vector.tensor_scalar_mul(s[:], score[:], 0.0625)
             else:
-                nc.scalar.mul(s[:], scores[u][:], 0.0625)
-            both = keep.tile([P, 2 * V], F32, name="both%d" % u, align_bytes=64)
+                nc.scalar.mul(s[:], score[:], 0.0625)
+            both = keep.tile([P, 2 * V], F32, name="both%d" % u, tag="both%d" % u, align_bytes=64)
             st, gate = both[:, 0:V], both[:, V : 2 * V]
-            other = keep.tile([P, V], F32, name="other%d" % u, align_bytes=64)
+            other = [keep.tile([P, HALF], F32, name="other%d%d" % (u, h), tag="other%d" % h, align_bytes=64) for h in range(2)]
             res = keep.tile([P, V], F32, name="res%d" % u, align_bytes=64)
             for h in range(2):
                 nc.scalar.activation(gate[:, halves[h]], s[:].indirect(lists[h]), ACT.Sigmoid)
             for vs in halves:
                 (nc.vector if u == 0 else nc.gpsimd).tensor_tensor(st[:, vs], s[:, vs], gate[:, vs], ALU.mult)
-            if u < PACK - 1:
-                nc.vector.tensor_copy(other[:], both[:].indirect(n2_t[:]))
-                nc.vector.tensor_tensor(res[:], st, other[:], ALU.max)
-                nc.sync.dma_start(rows[:, u, :], res[:])
-            else:
-                for h in range(2):
-                    nc.vector.tensor_copy(other[:, halves[h]], both[:].indirect(lists[h]))
-                for h in range(2):
-                    nc.vector.tensor_tensor(res[:, halves[h]], st[:, halves[h]], other[:, halves[h]], ALU.max)
-                    nc.sync.dma_start(rows[:, u, halves[h]], res[:, halves[h]])
+            for h in range(2):
+                nc.vector.tensor_copy(other[h][:], both[:].indirect(lists[h]))
+            for h in range(2):
+                nc.vector.tensor_tensor(res[:, halves[h]], st[:, halves[h]], other[h][:], ALU.max)
+            for c in range(4):
+                nc.sync.dma_start(rows[u, c], res[c:P:4, :])

@@ -20,6 +20,7 @@ PACK = 4
 BANK = 512
 CHUNKS = ((0, 256), (256, 128), (384, 128))
 HALF = V // 2
+TOK_FETCHES = ((0, 768), (768, 1024))
 TOK_PARTS = ((0, 512), (512, 768), (768, 1024))
 W_PARTS = ((0, 192), (192, 384), (384, 512))
 
@@ -77,8 +78,8 @@ def tile_picked_candprmstwicp_none_p_kernel(tc, x_words, x_scales, w1, gs, offs,
         quantize_w(0)
 
         tok_codes = []
-        for h, (j0, j1) in enumerate(TOK_PARTS):
-            codes = keep.tile([P, j1 - j0], U32, name="tok_codes%d" % h, tag=("tok_codes0", "tok_codes1", "w_raw384")[h], align_bytes=64)
+        for h, (j0, j1) in enumerate(TOK_FETCHES):
+            codes = keep.tile([P, j1 - j0], U32, name="tok_codes%d" % h, tag=("tok_codes0", "w_raw384")[h], align_bytes=64)
             nc.vector.tensor_copy(codes[:], x_codes[:].bitcast(U32).indirect(offs_t[:, j0 // 16 : j1 // 16]))
             tok_codes.append(codes)
         quantize_w(1)
@@ -98,13 +99,14 @@ def tile_picked_candprmstwicp_none_p_kernel(tc, x_words, x_scales, w1, gs, offs,
             sq = keep.tile([P, S], F32, name="sq%d" % t, tag="sq%d" % t, align_bytes=64)
             for h in range(2):
                 acc = psum.tile([P, BANK], F32, name="acc", tag="acc", bufs=5)
-                for codes, (j0, j1) in zip(tok_codes, TOK_PARTS):
+                for j0, j1 in TOK_PARTS:
+                    codes = tok_codes[0][:, j0:j1] if j1 <= 768 else tok_codes[1][:]
                     if j0 // BANK == h:
                         nc.tensor.matmul_mx(
                             out=acc[:, j0 - BANK * h : j1 - BANK * h],
                             lhsT=w_codes[:, cols].bitcast(FP8X4),
                             lhsT_scale=w_scales[:, cols],
-                            rhs=codes[:].bitcast(FP8X4),
+                            rhs=codes.bitcast(FP8X4),
                             rhs_scale=tok_scales[:, j0:j1],
                             start=True,
                             stop=True,
@@ -138,7 +140,6 @@ def tile_picked_candprmstwicp_none_p_kernel(tc, x_words, x_scales, w1, gs, offs,
                     if v0 <= c0 < v0 + n:
                         target = planes[c][:, t // 2, :, t % 2] if c < len(planes) else z_bfs[c][:, :, t]
                         nc.scalar.activation(target, roots[t][:, c0 : c0 + cn], ACT.Copy, scale=gain[:, t : t + 1])
-        nc.scalar.activation(warm[:, 2:3], planes[-1][:, 1, 0, 0:1], ACT.Sigmoid)
         z_mx = []
         for c, (v0, n) in enumerate(CHUNKS):
             z_bf = z_bfs[c]
@@ -170,7 +171,7 @@ def tile_picked_candprmstwicp_none_p_kernel(tc, x_words, x_scales, w1, gs, offs,
                     start=True,
                     stop=True,
                 )
-            s = keep.tile([P, V], F32, name="s%d" % u, tag=("z_bf2", "s1", "z_bf2", "both0")[u], align_bytes=64)
+            s = keep.tile([P, V], F32, name="s%d" % u, tag=("z_bf2", "s1", "z_bf2", "st0")[u], align_bytes=64)
             if u == 0:
                 cut = CHUNKS[-1][0]
                 nc.vector.tensor_scalar_mul(s[:, 0:cut], score[:, 0:cut], 0.0625)
@@ -179,8 +180,8 @@ def tile_picked_candprmstwicp_none_p_kernel(tc, x_words, x_scales, w1, gs, offs,
                 nc.vector.tensor_scalar_mul(s[:], score[:], 0.0625)
             else:
                 nc.scalar.mul(s[:], score[:], 0.0625)
-            both = keep.tile([P, 2 * V], F32, name="both%d" % u, tag="both%d" % u, align_bytes=64)
-            st, gate = both[:, 0:V], both[:, V : 2 * V]
+            st = keep.tile([P, V], F32, name="st%d" % u, tag="st%d" % u, align_bytes=64)
+            gate = keep.tile([P, V], F32, name="gate%d" % u, tag="gate%d" % u, align_bytes=64)
             other = [keep.tile([P, HALF], F32, name="other%d%d" % (u, h), tag="other%d" % h, align_bytes=64) for h in range(2)]
             res = keep.tile([P, V], F32, name="res%d" % u, align_bytes=64)
             for h in range(2):
@@ -188,7 +189,7 @@ def tile_picked_candprmstwicp_none_p_kernel(tc, x_words, x_scales, w1, gs, offs,
             for vs in halves:
                 (nc.vector if u == 0 else nc.gpsimd).tensor_tensor(st[:, vs], s[:, vs], gate[:, vs], ALU.mult)
             for h in range(2):
-                nc.vector.tensor_copy(other[h][:], both[:].indirect(lists[h]))
+                nc.vector.tensor_copy(other[h][:], st[:].indirect(lists[h]))
             for h in range(2):
                 nc.vector.tensor_tensor(res[:, halves[h]], st[:, halves[h]], other[h][:], ALU.max)
             for c in range(4):

@@ -39,11 +39,8 @@ def tile_picked_candprmstwicp_none_p_kernel(tc, x_words, x_scales, w1, gs, offs,
         x_codes = keep.tile([P, T], I32, name="x_codes", tag="x_codes", align_bytes=64)
         w_raw = [keep.tile([P, PACK, c1 - c0], F32, name="w_raw%d" % c0, tag="w_raw%d" % c0, align_bytes=64) for c0, c1 in W_PARTS]
         gain = keep.tile([P, PACK], F32, name="gain")
-        warm = keep.tile([P, 8], F32, name="warm")
 
         nc.vector.memset(x_bytes[:].bitcast(I32), 0)
-        nc.gpsimd.memset(warm[:], 1.0)
-        nc.scalar.activation(warm[:, 1:2], warm[:, 0:1], ACT.Sqrt)
         nc.sync.dma_start(offs_t[:], offs)
         nc.sync.dma_start(cand_t[:], cand)
         for q in range(4):

from contextlib import ExitStack

import concourse.mybir as mybir

K, T, S, V, H, C = 512, 2048, 1024, 512, 512, 512
FLOPS = 2 * K * H * S + 2 * H * C * V

F32 = mybir.dt.float32
BF16 = mybir.dt.bfloat16
I32 = mybir.dt.int32
U32 = mybir.dt.uint32
U16 = mybir.dt.uint16
U8 = mybir.dt.uint8
FP8X4 = mybir.dt.float8_e4m3fn_x4
ACT = mybir.ActivationFunctionType
ALU = mybir.AluOpType

P = 128
PACK = 4
BANK = 512
CHUNKS = ((0, 256), (256, 128), (384, 128))
HALF = V // 2
TOK_FETCHES = ((0, 768), (768, 1024))
TOK_PARTS = ((0, 512), (512, 768), (768, 1024))
W_PARTS = ((0, 192), (192, 384), (384, 512))


def tile_picked_candprmstwicp_none_p_kernel(tc, x_words, x_scales, w1, gs, offs, n1, cand, n2, out):
    nc = tc.nc
    with ExitStack() as ctx:
        keep = ctx.enter_context(tc.tile_pool(name="keep", bufs=1))
        psum = ctx.enter_context(tc.psum_pool(name="psum", bufs=1))

        offs_t = keep.tile([P, S // 16], U16, name="offs_t")
        cand_t = keep.tile([P, C // 16], U16, name="cand_t")
        n1_t = keep.tile([P, S // 16], U16, name="n1_t")
        n2_t = keep.tile([P, V // 16], U16, name="n2_t")
        x_bytes = keep.tile([P, T], U8, name="x_bytes", align_bytes=64)
        x_codes = keep.tile([P, T], I32, name="x_codes", tag="x_codes", align_bytes=64)
        w_raw = [keep.tile([P, PACK, c1 - c0], F32, name="w_raw%d" % c0, tag="w_raw%d" % c0, align_bytes=64) for c0, c1 in W_PARTS]
        gain = keep.tile([P, PACK], F32, name="gain")

        nc.vector.memset(x_bytes[:].bitcast(I32), 0)
        nc.sync.dma_start(offs_t[:], offs)
        nc.sync.dma_start(cand_t[:], cand)
        for q in range(4):
            nc.sync.dma_start(x_bytes[32 * q : 32 * q + 4, :].bitcast(I32), x_scales[0, 4 * q : 4 * q + 4, :].bitcast(I32))
        w_rows = w1.rearrange("(p j) c -> p j c", j=PACK)
        for i, (c0, c1) in enumerate(W_PARTS):
            nc.sync.dma_start(w_raw[i][:], w_rows[:, :, c0:c1])
            if i == 0:
                nc.sync.dma_start(x_codes[:], x_words[0].rearrange("p n r -> p (n r)").bitcast(I32))
        nc.sync.dma_start(n1_t[:], n1)
        nc.sync.dma_start(gain[:], gs.rearrange("(p t) o -> p (t o)", t=PACK))
        nc.sync.dma_start(n2_t[:], n2)

        tok_scales = keep.tile([P, S], U8, name="tok_scales", align_bytes=64)
        nc.vector.tensor_copy(tok_scales[:], x_bytes[:].indirect(offs_t[:]))
        cand_bytes = keep.tile([P, C], U8, name="cand_bytes", align_bytes=64)
        nc.vector.tensor_copy(cand_bytes[:], x_bytes[:].indirect(cand_t[:]))

        w_bf = keep.tile([P, PACK * H], BF16, name="w_bf", tag="w_bf", align_bytes=64)
        w_dealt = w_bf[:].rearrange("p (t m j) -> p m j t", t=PACK, j=PACK)
        for i, (c0, c1) in enumerate(W_PARTS):
            nc.scalar.copy(w_dealt[:, c0 // PACK : c1 // PACK], w_raw[i][:].rearrange("p j (m t) -> p m j t", t=PACK))
        w_codes = keep.tile([P, H], U32, name="w_codes", align_bytes=64)
        w_scales = keep.tile([P, H], U8, name="w_scales", align_bytes=64)

        def quantize_w(h):
            cols = slice(H // 2 * h, H // 2 * (h + 1))
            nc.vector.quantize_mx(
                out=w_codes[:, cols].bitcast(FP8X4), scales=w_scales[:, cols], in_=w_bf[:, 2 * H * h : 2 * H * (h + 1)]
            )

        quantize_w(0)

        tok_codes = []
        for h, (j0, j1) in enumerate(TOK_FETCHES):
            codes = keep.tile([P, j1 - j0], U32, name="tok_codes%d" % h, tag=("tok_codes0", "w_raw384")[h], align_bytes=64)
            nc.vector.tensor_copy(codes[:], x_codes[:].bitcast(U32).indirect(offs_t[:, j0 // 16 : j1 // 16]))
            tok_codes.append(codes)
        quantize_w(1)
        cand_codes = keep.tile([P, C], U32, name="cand_codes", tag="w_bf", align_bytes=64)
        nc.vector.tensor_copy(
            cand_codes[:].rearrange("p (u a c) -> p a u c", u=PACK, c=4), x_codes[:].bitcast(U32).indirect(cand_t[:])
        )
        cand_scales = keep.tile([P, C], U8, name="cand_scales", tag="x_codes", align_bytes=64)
        nc.vector.tensor_copy(
            cand_scales[:].bitcast(I32).rearrange("p (u a) -> p u a", u=PACK),
            cand_bytes[:].bitcast(I32).rearrange("p (a u) -> p u a", u=PACK),
        )

        squares = []
        for t in range(PACK):
            cols = slice(P * t, P * t + P)
            sq = keep.tile([P, S], F32, name="sq%d" % t, tag="sq%d" % t, align_bytes=64)
            for h in range(2):
                acc = psum.tile([P, BANK], F32, name="acc", tag="acc", bufs=5)
                for j0, j1 in TOK_PARTS:
                    codes = tok_codes[0][:, j0:j1] if j1 <= 768 else tok_codes[1][:]
                    if j0 // BANK == h:
                        nc.tensor.matmul_mx(
                            out=acc[:, j0 - BANK * h : j1 - BANK * h],
                            lhsT=w_codes[:, cols].bitcast(FP8X4),
                            lhsT_scale=w_scales[:, cols],
                            rhs=codes.bitcast(FP8X4),
                            rhs_scale=tok_scales[:, j0:j1],
                            start=True,
                            stop=True,
                        )
                nc.scalar.activation(sq[:, BANK * h : BANK * h + BANK], acc[:], ACT.Square)
            squares.append(sq)

        planes = [keep.tile([P, 2, n, 2], BF16, name="planes%d" % c, align_bytes=64) for c, (v0, n) in enumerate(CHUNKS)]
        z_bfs = [keep.tile([P, n, PACK], BF16, name="z_bf%d" % c, tag="z_bf%d" % c, align_bytes=64) for c, (v0, n) in enumerate(CHUNKS)]
        sums = [keep.tile([P, V], F32, name="ms%d" % t, align_bytes=64) for t in range(PACK)]
        roots = [
            keep.tile([P, V], F32, name="root%d" % t, tag="w_raw384" if t == 0 else "root%d" % t, align_bytes=64)
            for t in range(PACK)
        ]
        order = [(0, 0), (0, 1), (1, 0), (1, 1), (2, 0), (3, 0), (3, 1), (2, 1)]
        for t, h in order:
            final = (t, h) == order[-1]
            lined = keep.tile([P, BANK], F32, name="lined%d%d" % (t, h), tag="lined30" if final else "lined%d%d" % (t, h), align_bytes=64)
            pairs = lined[:].rearrange("p (v e) -> p v e", e=2)
            pieces = CHUNKS[1:] if final else ((HALF * h, HALF),)
            for v0, n in pieces:
                u0 = v0 - HALF * h
                nc.vector.tensor_copy(lined[:, 2 * u0 : 2 * (u0 + n)], squares[t][:].indirect(n1_t[:, v0 // 8 : (v0 + n) // 8]))
            for v0, n in pieces:
                vs = slice(v0, v0 + n)
                us = slice(v0 - HALF * h, v0 - HALF * h + n)
                adder = nc.vector if final and v0 + n == V else nc.gpsimd
                adder.tensor_tensor(sums[t][:, vs], pairs[:, us, 0], pairs[:, us, 1], ALU.add)
                nc.scalar.activation(roots[t][:, vs], sums[t][:, vs], ACT.Sqrt, bias=0.1)
                for c, (c0, cn) in enumerate(CHUNKS):
                    if v0 <= c0 < v0 + n:
                        target = planes[c][:, t // 2, :, t % 2] if c < len(planes) else z_bfs[c][:, :, t]
                        nc.scalar.activation(target, roots[t][:, c0 : c0 + cn], ACT.Copy, scale=gain[:, t : t + 1])
        z_mx = []
        for c, (v0, n) in enumerate(CHUNKS):
            z_bf = z_bfs[c]
            if c < len(planes):
                nc.vector.tensor_copy(
                    z_bf[:].rearrange("p v t -> p (v t)").bitcast(F32).rearrange("p (c i u) -> p c u i", i=4, u=2),
                    planes[c][:].rearrange("p u v e -> p (u v e)").bitcast(F32).rearrange("p (u c i) -> p c u i", i=4, u=2),
                )
            z_codes = keep.tile([P, n], U32, name="z_codes%d" % c, align_bytes=64)
            z_scales = keep.tile([P, n], U8, name="z_scales%d" % c, align_bytes=64)
            nc.vector.quantize_mx(
                out=z_codes[:].bitcast(FP8X4), scales=z_scales[:], in_=z_bf[:].rearrange("p v t -> p (v t)")
            )
            z_mx.append((z_codes, z_scales))
        rows = out.rearrange("(a u c) v -> u c a v", u=PACK, c=4)
        halves = [slice(0, HALF), slice(HALF, V)]
        lists = [n2_t[:, 0 : HALF // 16], n2_t[:, HALF // 16 : V // 16]]
        late = psum.tile([P, V], F32, name="late", tag="late")
        for u in range(PACK):
            cols = slice(P * u, P * u + P)
            score = psum.tile([P, V], F32, name="score%d" % u, tag=("first", "second", "late", "first")[u])
            for (v0, n), (z_codes, z_scales) in zip(CHUNKS, z_mx):
                nc.tensor.matmul_mx(
                    out=(late if (u, v0 + n) == (0, V) else score)[:, v0 : v0 + n],
                    lhsT=cand_codes[:, cols].bitcast(FP8X4),
                    lhsT_scale=cand_scales[:, cols],
                    rhs=z_codes[:].bitcast(FP8X4),
                    rhs_scale=z_scales[:],
                    start=True,
                    stop=True,
                )
            s = keep.tile([P, V], F32, name="s%d" % u, tag=("z_bf2", "s1", "z_bf2", "st0")[u], align_bytes=64)
            if u == 0:
                cut = CHUNKS[-1][0]
                nc.vector.tensor_scalar_mul(s[:, 0:cut], score[:, 0:cut], 0.0625)
                nc.vector.tensor_scalar_mul(s[:, cut:V], late[:, cut:V], 0.0625)
            elif u == 1:
                nc.vector.tensor_scalar_mul(s[:], score[:], 0.0625)
            else:
                nc.scalar.mul(s[:], score[:], 0.0625)
            st = keep.tile([P, V], F32, name="st%d" % u, tag="st%d" % u, align_bytes=64)
            gate = keep.tile([P, V], F32, name="gate%d" % u, tag="gate%d" % u, align_bytes=64)
            other = [keep.tile([P, HALF], F32, name="other%d%d" % (u, h), tag="other%d" % h, align_bytes=64) for h in range(2)]
            res = keep.tile([P, V], F32, name="res%d" % u, align_bytes=64)
            for h in range(2):
                nc.scalar.activation(gate[:, halves[h]], s[:].indirect(lists[h]), ACT.Sigmoid)
            for vs in halves:
                (nc.vector if u == 0 else nc.gpsimd).tensor_tensor(st[:, vs], s[:, vs], gate[:, vs], ALU.mult)
            for h in range(2):
                nc.vector.tensor_copy(other[h][:], st[:].indirect(lists[h]))
            for h in range(2):
                nc.vector.tensor_tensor(res[:, halves[h]], st[:, halves[h]], other[h][:], ALU.max)
            for c in range(4):
                nc.sync.dma_start(rows[u, c], res[c:P:4, :])
